import numpy as np
import ml_dtypes


def mxq(x, axis, fmt="e4m3"):
    dtype, down = {"e4m3": (ml_dtypes.float8_e4m3fn, 7), "e5m2": (ml_dtypes.float8_e5m2, 14)}[fmt]
    v = np.moveaxis(np.asarray(x, np.float32).astype(ml_dtypes.bfloat16).astype(np.float64), axis, -1)
    blocks = v.reshape(v.shape[:-1] + (-1, 32))
    amax = np.abs(blocks).max(-1, keepdims=True)
    byte = np.maximum(np.where(amax > 0, np.frexp(amax)[1] - 1 + 127, 0) - down, 1)
    scale = np.exp2(byte - 127.0)
    codes = (blocks / scale).astype(np.float32).astype(dtype).astype(np.float64)
    return np.moveaxis((codes * scale).reshape(v.shape), -1, axis)


WIDE = False


def mx_kscale(k):
    if not WIDE:
        return np.ones(k)
    levels = np.array([10, -10, 5, -5, 0])
    if k % 512:
        return np.exp2(np.random.permutation(np.resize(levels, k // 32))).repeat(32)
    a = np.empty((k // 512, 16))
    for p in range(k // 512):
        a[p, :8] = np.random.permutation(np.resize(levels, 8))
        for g in range(8):
            far = levels[np.abs(levels - a[p, g]) >= 10]
            a[p, g + 8] = far[np.random.randint(len(far))]
    return np.exp2(a.ravel()).repeat(32)


def f64(x):
    return np.asarray(x).astype(np.float64)


def striped8(idx):
    return np.asarray(idx).reshape(8, -1, 16).transpose(0, 2, 1).reshape(128, -1).astype(np.uint16)


def unstriped8(offs):
    return offs.reshape(8, 16, -1).transpose(0, 2, 1).reshape(8, -1).astype(np.int64)


def pick8(x, idx, run):
    r = np.arange(len(x))
    return x[r[:, None], idx[r % (8 * run) // run]]


E2M1 = np.array([0.0, 0.5, 1.0, 1.5, 2.0, 3.0, 4.0, 6.0, -0.0, -0.5, -1.0, -1.5, -2.0, -3.0, -4.0, -6.0])


def pack_weight(w, fmt):
    k, n = w.shape
    w = f64(np.asarray(w, np.float32).astype(ml_dtypes.bfloat16)).reshape(k // 32, 32, n)
    amax = np.abs(w).max(1)
    if fmt == "e4m3":
        byte = np.frexp(amax)[1] - 1 + 127 - 7
    else:
        mant, ex = np.frexp(amax / 6.0)
        byte = np.where(mant > 0.5, ex, ex - 1) + 127
    byte = np.clip(np.where(amax > 0, byte, 1), 1, 254)
    scaled = (w * np.exp2(127.0 - byte)[:, None, :]).reshape(k, n).astype(np.float32)
    by_word = np.ascontiguousarray(scaled.reshape(k // 512, 128, 4, n).transpose(0, 1, 3, 2))
    if fmt == "e4m3":
        words = by_word.astype(ml_dtypes.float8_e4m3fn).view(np.uint8)
    else:
        c = by_word.astype(ml_dtypes.float4_e2m1fn).view(np.uint8) & 0xF
        words = (c[..., 0::2] | (c[..., 1::2] << 4)).reshape(k // 512, 128, 2 * n)
    return np.ascontiguousarray(words), np.ascontiguousarray(byte.astype(np.uint8).reshape(k // 512, 16, n))


def unpack_weight(words, scales, fmt):
    g, _, n = scales.shape
    words = np.ascontiguousarray(words).reshape(g, 128, n, -1)
    if fmt == "e4m3":
        vals = words.view(ml_dtypes.float8_e4m3fn).astype(np.float64)
    else:
        nib = np.empty((g, 128, n, 4), np.uint8)
        nib[..., 0::2] = words & 0xF
        nib[..., 1::2] = words >> 4
        vals = E2M1[nib]
    vals = vals * np.repeat(np.exp2(scales.astype(np.float64) - 127.0), 8, axis=1)[..., None]
    return vals.transpose(0, 1, 3, 2).reshape(g * 512, n)


def sigmoid(v):
    return 1.0 / (1.0 + np.exp(-v))


D, E, T, Q, I = 512, 512, 1024, 128, 512


def setup_inputs():
    n = np.random.standard_normal
    idx = np.stack([np.random.permutation(T)[:I] for _ in range(8)])
    fd = mx_kscale(D)
    fe = mx_kscale(E)
    keysp = pack_weight(n((D, T)) / fd[:, None], "e2m1")
    return {
        "query": (n((D, Q)) * 0.4 / np.sqrt(D) * fd[:, None]).astype(np.float32),
        "keys_words": keysp[0],
        "keys_scales": keysp[1],
        "gout": (n((E, Q)) * 1 / np.sqrt(E) * fe[:, None]).astype(np.float32),
        "vals": (n((E, T)) / fe[:, None]).astype(np.float32),
        "steep": (np.random.uniform(2.0, 5.0, (Q, 1))).astype(np.float32),
        "boost": (np.random.uniform(0.5, 2.0, (1, I))).astype(np.float32),
        "fac": (np.random.uniform(0.5, 2.0, (1, T))).astype(np.float32),
        "dquery": (n((D, Q)) * 1.0 / np.sqrt(D) * fd[:, None]).astype(np.float32),
        "base": (0.5 * n((Q, T))).astype(np.float32),
        "offs": striped8(idx),
    }


def reference(query, keys_words, keys_scales, gout, vals, steep, boost, fac, dquery, base, offs):
    idx = unstriped8(offs)
    keysu = unpack_weight(keys_words, keys_scales, "e2m1")
    queryq = mxq(f64(query), 0, "e4m3")
    a = queryq.T @ keysu
    dqueryq = mxq(f64(dquery), 0, "e4m3")
    ta = dqueryq.T @ keysu
    b = sigmoid(pick8(a, idx, 16) * f64(steep))
    bb = b * f64(boost)
    bf = np.zeros((Q, T))
    bf[np.arange(Q)[:, None], idx[np.arange(Q) % 128 // 16]] = bb
    s = a + bf
    p = np.exp(s - np.max(s, axis=1, keepdims=True))
    z = np.sum(p, axis=1, keepdims=True)
    goutq = mxq(f64(gout), 0, "e4m3")
    valsq = mxq(f64(vals), 0, "e4m3")
    c0 = goutq.T @ valsq
    dz = np.sum(c0 * p * f64(fac) / np.square(z) * (-1.0), axis=1, keepdims=True)
    dp = c0 / z * f64(fac) + dz
    ds = dp * p
    dbb = pick8(ds, idx, 16)
    db = dbb * f64(boost)
    xb = pick8(ta, idx, 16) * f64(steep) * b * (1.0 - b)
    xbb = xb * f64(boost)
    xbf = np.zeros((Q, T))
    xbf[np.arange(Q)[:, None], idx[np.arange(Q) % 128 // 16]] = xbb
    xs = ta + xbf
    xp = xs * p
    xz = np.sum(xp, axis=1, keepdims=True)
    xdz = np.sum((xp * f64(fac) * c0 - xz * z * 2.0 * c0 * p * f64(fac) / np.square(z)) / np.square(z) * (-1.0), axis=1, keepdims=True)
    xdp = xz * c0 / np.square(z) * (-1.0) * f64(fac) + xdz
    xds = xdp * p + xp * dp
    xdbb = pick8(xds, idx, 16)
    xdb = xdbb * f64(boost)
    xe1 = ((xdb * b + xb * db) * (1.0 - b) + xb * (-1.0) * db * b) * f64(steep)
    xs1 = np.zeros((Q, T))
    xs1[np.arange(Q)[:, None], idx[np.arange(Q) % 128 // 16]] = xe1
    xda = xds + xs1
    y = xda * 1024.0 + f64(base)
    return y

@@ -1,0 +1,250 @@
+from contextlib import ExitStack
+
+import concourse.mybir as mybir
+from concourse.masks import make_identity
+
+D, E, T, Q, I = 512, 512, 1024, 128, 512
+FLOPS = 3 * 2 * 512 * Q * T
+
+F32 = mybir.dt.float32
+BF16 = mybir.dt.bfloat16
+U32 = mybir.dt.uint32
+I32 = mybir.dt.int32
+U16 = mybir.dt.uint16
+U8 = mybir.dt.uint8
+FP8X4 = mybir.dt.float8_e4m3fn_x4
+FP4X4 = mybir.dt.float4_e2m1fn_x4
+ALU = mybir.AluOpType
+ACT = mybir.ActivationFunctionType
+AX = mybir.AxisListType
+
+P = 128
+PACK = 4
+BANK = 512
+NB = T // BANK
+BLK = BANK // P
+CH = 256
+NCH = T // CH
+HALF = I // 2
+
+
+def tile_attend_hvboost_heads_kernel(tc, query, keys_words, keys_scales, gout, vals, steep, boost, fac, dquery, base, offs, out):
+    nc = tc.nc
+    V, S, G, PE = nc.vector, nc.scalar, nc.gpsimd, nc.tensor
+    with ExitStack() as ctx:
+        sb = ctx.enter_context(tc.tile_pool(name="sb", bufs=1))
+        ps = ctx.enter_context(tc.psum_pool(name="ps", bufs=1))
+
+        def banks(tag):
+            return [ps.tile([P, BANK], F32, name="%s%d" % (tag, h), tag="%s%d" % (tag, h)) for h in range(NB)]
+
+        def f32(name, width):
+            return sb.tile([P, width], F32, name=name)
+
+        def interleave(copy, dst, src):
+            copy(dst.rearrange("p (c i) t -> p c t i", i=4), src.rearrange("p t (c i) -> p c t i", i=4))
+
+        def load_rows(name, rows, width):
+            raw = sb.tile([P, PACK, width], F32, name=name)
+            nc.sync.dma_start(out=raw[:], in_=rows.rearrange("(p j) w -> p j w", j=PACK))
+            return raw
+
+        def quantise(name, copy, raw, width):
+            grouped = sb.tile([P, width, PACK], BF16, name=name + "_bf", align_bytes=64)
+            codes = sb.tile([P, width], U32, name=name + "_codes", align_bytes=64)
+            scales = sb.tile([P, width], U8, name=name + "_scales", align_bytes=64)
+            interleave(copy, grouped[:], raw[:])
+            V.quantize_mx(out=codes[:].bitcast(FP8X4), scales=scales[:], in_=grouped[:].rearrange("p w j -> p (w j)"))
+            return codes, scales
+
+        def turn(dst, src, start=True, stop=True):
+            for j in range(T // P):
+                h, c = divmod(j, BLK)
+                PE.matmul(dst[h][:, c * P:(c + 1) * P], lhsT=src[:, j * P:(j + 1) * P], rhs=ident[:], is_transpose=True,
+                          start=(start and c == 0), stop=(stop and c == BLK - 1))
+
+        def halves(tile):
+            return [tile[:, h * BANK:(h + 1) * BANK] for h in range(NB)]
+
+        kscale = sb.tile([P, T], U8, name="kscale", align_bytes=64)
+        V.memset(kscale[:].bitcast(I32), 0)
+        q_raw = load_rows("q_raw", query, Q)
+        kwords = sb.tile([P, 2 * T], U8, name="kwords", align_bytes=64)
+        nc.sync.dma_start(out=kwords[:].bitcast(I32), in_=keys_words[0].bitcast(I32))
+        for r in range(4):
+            nc.sync.dma_start(out=kscale[32 * r:32 * r + 4, :].bitcast(I32), in_=keys_scales[0, 4 * r:4 * r + 4, :].bitcast(I32))
+        dq_raw = load_rows("dq_raw", dquery, Q)
+        offsets = sb.tile([P, I // 16], U16, name="offsets")
+        nc.sync.dma_start(offsets[:], offs)
+        boost_c = f32("boost_c", PACK)
+        nc.sync.dma_start(out=boost_c[:], in_=boost[0].rearrange("(p c) -> p c", c=PACK))
+        steep_c = f32("steep_c", 1)
+        nc.sync.dma_start(out=steep_c[:], in_=steep)
+        go_raw = load_rows("go_raw", gout, Q)
+        v_raw = [load_rows("v_raw%d" % c, vals[:, c * CH:(c + 1) * CH], CH) for c in range(NCH)]
+        ident = f32("ident", P)
+        make_identity(nc, ident[:])
+        fac_rows = f32("fac_rows", P)
+        G.memset(fac_rows[:], 0.0)
+        nc.sync.dma_start(out=fac_rows[0:T // P, :], in_=fac[0].rearrange("(j p) -> j p", p=P))
+        base_sb = f32("base_sb", T)
+        nc.sync.dma_start(out=base_sb[:], in_=base)
+
+        warm = f32("warm", 1)
+        V.memset(warm[:], 0.0)
+        warm_out = f32("warm_out", 1)
+        S.activation(warm_out[:], warm[:], ACT.Exp)
+        bf, xbf, xs1 = f32("bf", T), f32("xbf", T), f32("xs1", T)
+        for window in (bf, xbf, xs1):
+            V.memset(window[:], 0.0)
+
+        def steep_times(name, factor):
+            col = f32(name, 1)
+            G.tensor_scalar(col[:], steep_c[:], factor, 0.0, ALU.mult, ALU.add)
+            return col
+
+        hsteep, qsteep, nqsteep, nsteep = (steep_times(n, f) for n, f in (("hsteep", 0.5), ("qsteep", 0.25), ("nqsteep", -0.25), ("nsteep", -1.0)))
+
+        def scores(codes, scales, dst):
+            for h in range(NB):
+                PE.matmul_mx(out=dst[h][:], lhsT=codes[:].bitcast(FP8X4), lhsT_scale=scales[:],
+                             rhs=kwords[:, 2 * h * BANK:2 * (h + 1) * BANK].bitcast(FP4X4), rhs_scale=kscale[:, h * BANK:(h + 1) * BANK],
+                             start=True, stop=True)
+
+        pa = banks("a")
+        scores(*quantise("q", V.tensor_copy, q_raw, Q), pa)
+        a_sb = f32("a_sb", T)
+        S.copy(halves(a_sb)[0], pa[0][:])
+        V.tensor_copy(halves(a_sb)[1], pa[1][:])
+        pc = banks("c")
+        for m in range(PACK):
+            PE.matmul(pc[0][:, m * P:(m + 1) * P], lhsT=boost_c[:, m:m + 1].to_broadcast([P, P]), rhs=ident[:], is_transpose=True,
+                      start=(m == 0), stop=(m == PACK - 1))
+        boost_b = f32("boost_b", I)
+        S.copy(boost_b[:].rearrange("p (n m) -> p n m", m=PACK), pc[0][:].rearrange("p (m n) -> p n m", m=PACK))
+        pb = banks("b")
+        scores(*quantise("dq", V.tensor_copy, dq_raw, Q), pb)
+
+        a_g, th, b = f32("a_g", I), f32("th", I), f32("b", I)
+        lists = [offsets[:, h * HALF // 16:(h + 1) * HALF // 16] for h in range(2)]
+        cols = [slice(h * HALF, (h + 1) * HALF) for h in range(2)]
+        for h in range(2):
+            V.tensor_copy(a_g[:, cols[h]], a_sb[:].indirect(lists[h]))
+        for h in range(2):
+            S.activation(th[:, cols[h]], a_g[:, cols[h]], ACT.Tanh, scale=hsteep[:])
+            S.activation(b[:, cols[h]], th[:, cols[h]], ACT.Copy, scale=0.5, bias=0.5)
+        for h in range(2):
+            V.tensor_tensor(bf[:].indirect(lists[h]), b[:, cols[h]], boost_b[:, cols[h]], ALU.mult)
+
+        ta_sb = f32("ta_sb", T)
+        for h in range(NB):
+            S.copy(halves(ta_sb)[h], pb[h][:])
+        sq, v = f32("sq", I), f32("v", I)
+        S.activation(sq[:], th[:], ACT.Square)
+        S.activation(v[:], sq[:], ACT.Identity, scale=nqsteep[:], bias=qsteep[:])
+        go_codes, go_scales = quantise("go", V.tensor_copy, go_raw, Q)
+        v_bf = [sb.tile([P, CH, PACK], BF16, name="v_bf%d" % c, align_bytes=64) for c in range(NCH)]
+        for c in range(2):
+            interleave(S.copy, v_bf[c][:], v_raw[c][:])
+
+        s = f32("s", T)
+        V.tensor_tensor(s[:], a_sb[:], bf[:], ALU.add)
+        nmax = f32("nmax", 1)
+        V.tensor_reduce(nmax[:], s[:], AX.X, ALU.max, negate=True)
+        p = sb.tile([P, T], F32, name="p", tag="v_raw1")
+        u = f32("u", I)
+        S.activation(p[:], s[:], ACT.Exp, bias=nmax[:], accum_out=u[:, 0:1])
+        S.activation(u[:, 1:2], u[:, 0:1], ACT.Copy, scale=-1.0)
+
+        ta_g = f32("ta_g", I)
+        V.tensor_copy(ta_g[:], ta_sb[:].indirect(offsets[:]))
+        for c in range(2, NCH):
+            interleave(V.tensor_copy, v_bf[c][:], v_raw[c][:])
+        v_codes = sb.tile([P, T], U32, name="v_codes", align_bytes=64)
+        v_scales = sb.tile([P, T], U8, name="v_scales", align_bytes=64)
+        for c in range(NCH):
+            V.quantize_mx(out=v_codes[:, c * CH:(c + 1) * CH].bitcast(FP8X4), scales=v_scales[:, c * CH:(c + 1) * CH],
+                          in_=v_bf[c][:].rearrange("p w j -> p (w j)"))
+        rzs = f32("rzs", 2)
+        rz, nrz = rzs[:, 0:1], rzs[:, 1:2]
+        V.reciprocal(rzs[:], u[:, 0:2])
+        V.tensor_tensor(u[:], v[:], boost_b[:], ALU.mult)
+        V.tensor_tensor(xbf[:].indirect(offsets[:]), ta_g[:], u[:], ALU.mult)
+
+        PE.matmul(pc[1][:, 0:P], lhsT=fac_rows[:], rhs=ident[:], is_transpose=True, start=True, stop=True)
+        fac_c = f32("fac_c", T // P)
+        S.copy(fac_c[:], pc[1][:, 0:T // P])
+        pa = banks("a")
+        gt = f32("gt", T)
+        for j in range(T // P):
+            h, c = divmod(j, BLK)
+            PE.matmul_mx(out=pa[h][:, c * P:(c + 1) * P], lhsT=v_codes[:, j * P:(j + 1) * P].bitcast(FP8X4), lhsT_scale=v_scales[:, j * P:(j + 1) * P],
+                         rhs=go_codes[:].bitcast(FP8X4), rhs_scale=go_scales[:], start=True, stop=True)
+        for j in range(T // P):
+            h, c = divmod(j, BLK)
+            S.activation(gt[:, j * P:(j + 1) * P], pa[h][:, c * P:(c + 1) * P], ACT.Copy, scale=fac_c[:, j:j + 1])
+        pg = banks("b")
+        turn(pg, gt)
+        npn = f32("npn", T)
+        S.activation(npn[:], p[:], ACT.Copy, scale=nrz)
+
+        pc = banks("c")
+        turn(pc, ta_sb)
+        tat = f32("tat", T)
+        for h in range(NB):
+            S.copy(halves(tat)[h], pc[h][:])
+        pxs = banks("d")
+        turn(pxs, tat, stop=False)
+        pa = banks("a")
+        turn(pa, xbf)
+        xbft = f32("xbft", T)
+        for h in range(NB):
+            S.copy(halves(xbft)[h], pa[h][:])
+        turn(pxs, xbft, start=False)
+
+        gp, ds, xp, t, xds = f32("gp", T), f32("ds", T), f32("xp", T), f32("t", T), f32("xds", T)
+        gsum = [f32("gsum%d" % h, 1) for h in range(NB)]
+        xsum = [f32("xsum%d" % h, 1) for h in range(NB)]
+        ksum = [f32("ksum%d" % h, 1) for h in range(NB)]
+        gs, xm, ks = f32("gs", 1), f32("xm", 1), f32("ks", 1)
+        for h in range(NB):
+            V.scalar_tensor_tensor(halves(gp)[h], pg[h][:], rz, halves(p)[h], ALU.mult, ALU.mult, accum_out=gsum[h][:])
+        S.activation(gs[:], gsum[0][:], ACT.Identity, bias=gsum[1][:])
+        w = f32("w", I)
+        V.scalar_tensor_tensor(w[:], th[:], nsteep[:], ta_g[:], ALU.mult, ALU.mult)
+        V.scalar_tensor_tensor(ds[:], npn[:], gs[:], gp[:], ALU.mult, ALU.add)
+        for h in range(NB):
+            V.scalar_tensor_tensor(halves(xp)[h], pxs[h][:], rz, halves(p)[h], ALU.mult, ALU.mult, accum_out=xsum[h][:])
+        S.activation(xm[:], xsum[0][:], ACT.Identity, bias=xsum[1][:])
+        e2 = f32("e2", I)
+        V.tensor_tensor(e2[:, cols[0]], ds[:].indirect(lists[0]), w[:, cols[0]], ALU.mult)
+        for h in range(NB):
+            V.scalar_tensor_tensor(halves(t)[h], pxs[h][:], xm[:], halves(ds)[h], ALU.subtract, ALU.mult, accum_out=ksum[h][:])
+        S.activation(ks[:], ksum[0][:], ACT.Identity, bias=ksum[1][:])
+        V.tensor_tensor(e2[:, cols[1]], ds[:].indirect(lists[1]), w[:, cols[1]], ALU.mult)
+        V.scalar_tensor_tensor(xds[:], npn[:], ks[:], t[:], ALU.mult, ALU.add)
+        e = f32("e", I)
+        for h in range(2):
+            V.tensor_tensor(e[:, cols[h]], xds[:].indirect(lists[h]), e2[:, cols[h]], ALU.add)
+        for h in range(2):
+            V.tensor_tensor(xs1[:].indirect(lists[h]), e[:, cols[h]], u[:, cols[h]], ALU.mult)
+
+        pc = banks("c")
+        turn(pc, base_sb)
+        baset = f32("baset", T)
+        for h in range(NB):
+            S.copy(halves(baset)[h], pc[h][:])
+        py = banks("b")
+        turn(py, baset, stop=False)
+        pa = banks("a")
+        turn(pa, xds)
+        xdst = f32("xdst", T)
+        for h in range(NB):
+            S.activation(halves(xdst)[h], pa[h][:], ACT.Copy, scale=1024.0)
+        turn(py, xdst, start=False)
+        res = f32("res", T)
+        for k in range(NCH):
+            h, c = divmod(k * CH, BANK)
+            piece = slice(k * CH, (k + 1) * CH)
+            V.scalar_tensor_tensor(res[:, piece], xs1[:, piece], 1024.0, py[h][:, c:c + CH], ALU.mult, ALU.add)
+            (nc.sync if k % 2 == 0 else nc.scalar).dma_start(out=out[:, piece], in_=res[:, piece])

@@ -36,16 +36,16 @@ def tile_attend_hvboost_heads_kernel(tc, query, keys_words, keys_scales, gout, v
         ps = ctx.enter_context(tc.psum_pool(name="ps", bufs=1))
 
         def banks(tag):
-            return [ps.tile([P, BANK], F32, name="%s%d" % (tag, h), tag="%s%d" % (tag, h)) for h in range(NB)]
+            return halves(ps.tile([P, NB * BANK], F32, name=tag))
 
-        def f32(name, width):
-            return sb.tile([P, width], F32, name=name)
+        def f32(name, width, tag=None):
+            return sb.tile([P, width], F32, name=name, tag=tag or name, align_bytes=64)
 
         def interleave(copy, dst, src):
             copy(dst.rearrange("p (c i) t -> p c t i", i=4), src.rearrange("p t (c i) -> p c t i", i=4))
 
         def load_rows(name, rows, width):
-            raw = sb.tile([P, PACK, width], F32, name=name)
+            raw = sb.tile([P, PACK, width], F32, name=name, align_bytes=64)
             nc.sync.dma_start(out=raw[:], in_=rows.rearrange("(p j) w -> p j w", j=PACK))
             return raw
 
@@ -66,6 +66,15 @@ def tile_attend_hvboost_heads_kernel(tc, query, keys_words, keys_scales, gout, v
         def halves(tile):
             return [tile[:, h * BANK:(h + 1) * BANK] for h in range(NB)]
 
+        def copy_out(name, src, scale=None, tag=None):
+            dst = f32(name, T, tag)
+            for h in range(NB):
+                if scale is None:
+                    S.copy(halves(dst)[h], src[h][:])
+                else:
+                    S.activation(halves(dst)[h], src[h][:], ACT.Copy, scale=scale)
+            return dst
+
         kscale = sb.tile([P, T], U8, name="kscale", align_bytes=64)
         V.memset(kscale[:].bitcast(I32), 0)
         q_raw = load_rows("q_raw", query, Q)
@@ -76,16 +85,17 @@ def tile_attend_hvboost_heads_kernel(tc, query, keys_words, keys_scales, gout, v
         dq_raw = load_rows("dq_raw", dquery, Q)
         offsets = sb.tile([P, I // 16], U16, name="offsets")
         nc.sync.dma_start(offsets[:], offs)
+        ident = f32("ident", P)
+        make_identity(nc, ident[:])
         boost_c = f32("boost_c", PACK)
         nc.sync.dma_start(out=boost_c[:], in_=boost[0].rearrange("(p c) -> p c", c=PACK))
         steep_c = f32("steep_c", 1)
         nc.sync.dma_start(out=steep_c[:], in_=steep)
-        go_raw = load_rows("go_raw", gout, Q)
-        v_raw = [load_rows("v_raw%d" % c, vals[:, c * CH:(c + 1) * CH], CH) for c in range(NCH)]
-        ident = f32("ident", P)
-        make_identity(nc, ident[:])
         fac_rows = f32("fac_rows", P)
         G.memset(fac_rows[:], 0.0)
+        v_raw = [load_rows("v_raw%d" % c, vals[:, c * CH:(c + 1) * CH], CH) for c in range(2)]
+        go_raw = load_rows("go_raw", gout, Q)
+        v_raw = v_raw + [load_rows("v_raw%d" % c, vals[:, c * CH:(c + 1) * CH], CH) for c in range(2, NCH)]
         nc.sync.dma_start(out=fac_rows[0:T // P, :], in_=fac[0].rearrange("(j p) -> j p", p=P))
         base_sb = f32("base_sb", T)
         nc.sync.dma_start(out=base_sb[:], in_=base)
@@ -100,148 +110,127 @@ def tile_attend_hvboost_heads_kernel(tc, query, keys_words, keys_scales, gout, v
 
         def steep_times(name, factor):
             col = f32(name, 1)
-            G.tensor_scalar(col[:], steep_c[:], factor, 0.0, ALU.mult, ALU.add)
+            S.activation(col[:], steep_c[:], ACT.Copy, scale=factor)
             return col
 
-        hsteep, qsteep, nqsteep, nsteep = (steep_times(n, f) for n, f in (("hsteep", 0.5), ("qsteep", 0.25), ("nqsteep", -0.25), ("nsteep", -1.0)))
-
-        def scores(codes, scales, dst):
-            for h in range(NB):
-                PE.matmul_mx(out=dst[h][:], lhsT=codes[:].bitcast(FP8X4), lhsT_scale=scales[:],
-                             rhs=kwords[:, 2 * h * BANK:2 * (h + 1) * BANK].bitcast(FP4X4), rhs_scale=kscale[:, h * BANK:(h + 1) * BANK],
+        def scores(codes, scales, dst, width):
+            for k, piece in enumerate(dst):
+                PE.matmul_mx(out=piece[:, 0:width], lhsT=codes[:].bitcast(FP8X4), lhsT_scale=scales[:],
+                             rhs=kwords[:, 2 * k * width:2 * (k + 1) * width].bitcast(FP4X4), rhs_scale=kscale[:, k * width:(k + 1) * width],
                              start=True, stop=True)
 
-        pa = banks("a")
-        scores(*quantise("q", V.tensor_copy, q_raw, Q), pa)
+        pa = banks("a") + banks("d")
+        scores(*quantise("q", V.tensor_copy, q_raw, Q), pa, CH)
         a_sb = f32("a_sb", T)
-        S.copy(halves(a_sb)[0], pa[0][:])
-        V.tensor_copy(halves(a_sb)[1], pa[1][:])
+        for k in range(NCH):
+            (S.copy if k % 2 == 0 else V.tensor_copy)(a_sb[:, k * CH:(k + 1) * CH], pa[k][:, 0:CH])
+        hboost_c = f32("hboost_c", PACK)
+        S.activation(hboost_c[:], boost_c[:], ACT.Copy, scale=0.5)
+        hsteep, nhsteep, nsteep = (steep_times(n, f) for n, f in (("hsteep", 0.5), ("nhsteep", -0.5), ("nsteep", -1.0)))
         pc = banks("c")
         for m in range(PACK):
-            PE.matmul(pc[0][:, m * P:(m + 1) * P], lhsT=boost_c[:, m:m + 1].to_broadcast([P, P]), rhs=ident[:], is_transpose=True,
+            PE.matmul(pc[0][:, m * P:(m + 1) * P], lhsT=hboost_c[:, m:m + 1].to_broadcast([P, P]), rhs=ident[:], is_transpose=True,
                       start=(m == 0), stop=(m == PACK - 1))
-        boost_b = f32("boost_b", I)
-        S.copy(boost_b[:].rearrange("p (n m) -> p n m", m=PACK), pc[0][:].rearrange("p (m n) -> p n m", m=PACK))
+        hboost = pc[0][:].rearrange("p (m n) -> p n m", m=PACK)
         pb = banks("b")
-        scores(*quantise("dq", V.tensor_copy, dq_raw, Q), pb)
+        scores(*quantise("dq", V.tensor_copy, dq_raw, Q), pb, BANK)
 
-        a_g, th, b = f32("a_g", I), f32("th", I), f32("b", I)
+        a_g, th, bb = f32("a_g", I), f32("th", I), f32("bb", I)
         lists = [offsets[:, h * HALF // 16:(h + 1) * HALF // 16] for h in range(2)]
         cols = [slice(h * HALF, (h + 1) * HALF) for h in range(2)]
+        quads = [slice(h * HALF // PACK, (h + 1) * HALF // PACK) for h in range(2)]
+
+        def by_quads(ap):
+            return ap.rearrange("p (n m) -> p n m", m=PACK)
+
         for h in range(2):
             V.tensor_copy(a_g[:, cols[h]], a_sb[:].indirect(lists[h]))
         for h in range(2):
             S.activation(th[:, cols[h]], a_g[:, cols[h]], ACT.Tanh, scale=hsteep[:])
-            S.activation(b[:, cols[h]], th[:, cols[h]], ACT.Copy, scale=0.5, bias=0.5)
         for h in range(2):
-            V.tensor_tensor(bf[:].indirect(lists[h]), b[:, cols[h]], boost_b[:, cols[h]], ALU.mult)
+            V.scalar_tensor_tensor(by_quads(bb[:, cols[h]]), by_quads(th[:, cols[h]]), 1.0, hboost[:, quads[h], :], ALU.add, ALU.mult)
+        V.tensor_copy(bf[:].indirect(offsets[:]), bb[:])
 
-        ta_sb = f32("ta_sb", T)
-        for h in range(NB):
-            S.copy(halves(ta_sb)[h], pb[h][:])
-        sq, v = f32("sq", I), f32("v", I)
+        ta_sb = copy_out("ta_sb", pb)
+        v_bf = sb.tile([P, T + Q, PACK], BF16, name="v_bf", tag="a_g", align_bytes=64)
+        interleave(S.copy, v_bf[:, T:, :], go_raw[:])
+        for c in range(NCH):
+            interleave(S.copy, v_bf[:, c * CH:(c + 1) * CH, :], v_raw[c][:])
+        pb = banks("b")
+        PE.matmul(pb[0][:, 0:P], lhsT=fac_rows[:], rhs=ident[:], is_transpose=True, start=True, stop=True)
+        nfac_c = f32("nfac_c", T // P, "v_raw2")
+        S.activation(nfac_c[:], pb[0][:, 0:T // P], ACT.Copy, scale=-1.0)
+        sq, v = f32("sq", I, "v_raw3"), f32("v", I)
         S.activation(sq[:], th[:], ACT.Square)
-        S.activation(v[:], sq[:], ACT.Identity, scale=nqsteep[:], bias=qsteep[:])
-        go_codes, go_scales = quantise("go", V.tensor_copy, go_raw, Q)
-        v_bf = [sb.tile([P, CH, PACK], BF16, name="v_bf%d" % c, align_bytes=64) for c in range(NCH)]
-        for c in range(2):
-            interleave(S.copy, v_bf[c][:], v_raw[c][:])
+        S.activation(v[:], sq[:], ACT.Identity, scale=nhsteep[:], bias=hsteep[:])
 
         s = f32("s", T)
         V.tensor_tensor(s[:], a_sb[:], bf[:], ALU.add)
         nmax = f32("nmax", 1)
         V.tensor_reduce(nmax[:], s[:], AX.X, ALU.max, negate=True)
-        p = sb.tile([P, T], F32, name="p", tag="v_raw1")
-        u = f32("u", I)
-        S.activation(p[:], s[:], ACT.Exp, bias=nmax[:], accum_out=u[:, 0:1])
-        S.activation(u[:, 1:2], u[:, 0:1], ACT.Copy, scale=-1.0)
+        p = f32("p", T, "v_raw3")
+        z = f32("z", 1)
+        S.activation(p[:], s[:], ACT.Exp, bias=nmax[:], accum_out=z[:])
 
+        codes = sb.tile([P, T + Q], U32, name="codes", tag="bf", align_bytes=64)
+        scales = sb.tile([P, T + Q], U8, name="scales", align_bytes=64)
+        v_codes, v_scales, go_codes, go_scales = codes[:, 0:T], scales[:, 0:T], codes[:, T:], scales[:, T:]
+        for piece in (slice(T, T + Q), slice(0, T)):
+            V.quantize_mx(out=codes[:, piece].bitcast(FP8X4), scales=scales[:, piece], in_=v_bf[:, piece, :].rearrange("p w j -> p (w j)"))
         ta_g = f32("ta_g", I)
         V.tensor_copy(ta_g[:], ta_sb[:].indirect(offsets[:]))
-        for c in range(2, NCH):
-            interleave(V.tensor_copy, v_bf[c][:], v_raw[c][:])
-        v_codes = sb.tile([P, T], U32, name="v_codes", align_bytes=64)
-        v_scales = sb.tile([P, T], U8, name="v_scales", align_bytes=64)
-        for c in range(NCH):
-            V.quantize_mx(out=v_codes[:, c * CH:(c + 1) * CH].bitcast(FP8X4), scales=v_scales[:, c * CH:(c + 1) * CH],
-                          in_=v_bf[c][:].rearrange("p w j -> p (w j)"))
-        rzs = f32("rzs", 2)
-        rz, nrz = rzs[:, 0:1], rzs[:, 1:2]
-        V.reciprocal(rzs[:], u[:, 0:2])
-        V.tensor_tensor(u[:], v[:], boost_b[:], ALU.mult)
+        rz = f32("rz", 1)
+        V.reciprocal(rz[:], z[:])
+        u = f32("u", I, "a_sb")
+        V.tensor_tensor(by_quads(u[:]), by_quads(v[:]), hboost, ALU.mult)
+        w = f32("w", I, "v")
+        V.scalar_tensor_tensor(w[:], th[:], nsteep[:], ta_g[:], ALU.mult, ALU.mult)
         V.tensor_tensor(xbf[:].indirect(offsets[:]), ta_g[:], u[:], ALU.mult)
 
-        PE.matmul(pc[1][:, 0:P], lhsT=fac_rows[:], rhs=ident[:], is_transpose=True, start=True, stop=True)
-        fac_c = f32("fac_c", T // P)
-        S.copy(fac_c[:], pc[1][:, 0:T // P])
         pa = banks("a")
         gt = f32("gt", T)
         for j in range(T // P):
             h, c = divmod(j, BLK)
             PE.matmul_mx(out=pa[h][:, c * P:(c + 1) * P], lhsT=v_codes[:, j * P:(j + 1) * P].bitcast(FP8X4), lhsT_scale=v_scales[:, j * P:(j + 1) * P],
-                         rhs=go_codes[:].bitcast(FP8X4), rhs_scale=go_scales[:], start=True, stop=True)
+                         rhs=go_codes.bitcast(FP8X4), rhs_scale=go_scales, start=True, stop=True)
         for j in range(T // P):
             h, c = divmod(j, BLK)
-            S.activation(gt[:, j * P:(j + 1) * P], pa[h][:, c * P:(c + 1) * P], ACT.Copy, scale=fac_c[:, j:j + 1])
-        pg = banks("b")
+            S.activation(gt[:, j * P:(j + 1) * P], pa[h][:, c * P:(c + 1) * P], ACT.Copy, scale=nfac_c[:, j:j + 1])
+        pg = banks("d")
         turn(pg, gt)
-        npn = f32("npn", T)
-        S.activation(npn[:], p[:], ACT.Copy, scale=nrz)
+        g = copy_out("g", pg)
+        pn = f32("pn", T, "gt")
+        S.activation(pn[:], p[:], ACT.Copy, scale=rz[:])
 
-        pc = banks("c")
-        turn(pc, ta_sb)
-        tat = f32("tat", T)
-        for h in range(NB):
-            S.copy(halves(tat)[h], pc[h][:])
-        pxs = banks("d")
-        turn(pxs, tat, stop=False)
         pa = banks("a")
-        turn(pa, xbf)
-        xbft = f32("xbft", T)
-        for h in range(NB):
-            S.copy(halves(xbft)[h], pa[h][:])
-        turn(pxs, xbft, start=False)
+        turn(pa, ta_sb, stop=False)
+        turn(pa, xbf, start=False)
+        xst = copy_out("xst", pa, scale=-1.0)
+        pxs = banks("b")
+        turn(pxs, xst)
+        xs = copy_out("xs", pxs)
 
         gp, ds, xp, t, xds = f32("gp", T), f32("ds", T), f32("xp", T), f32("t", T), f32("xds", T)
-        gsum = [f32("gsum%d" % h, 1) for h in range(NB)]
-        xsum = [f32("xsum%d" % h, 1) for h in range(NB)]
-        ksum = [f32("ksum%d" % h, 1) for h in range(NB)]
         gs, xm, ks = f32("gs", 1), f32("xm", 1), f32("ks", 1)
-        for h in range(NB):
-            V.scalar_tensor_tensor(halves(gp)[h], pg[h][:], rz, halves(p)[h], ALU.mult, ALU.mult, accum_out=gsum[h][:])
-        S.activation(gs[:], gsum[0][:], ACT.Identity, bias=gsum[1][:])
-        w = f32("w", I)
-        V.scalar_tensor_tensor(w[:], th[:], nsteep[:], ta_g[:], ALU.mult, ALU.mult)
-        V.scalar_tensor_tensor(ds[:], npn[:], gs[:], gp[:], ALU.mult, ALU.add)
-        for h in range(NB):
-            V.scalar_tensor_tensor(halves(xp)[h], pxs[h][:], rz, halves(p)[h], ALU.mult, ALU.mult, accum_out=xsum[h][:])
-        S.activation(xm[:], xsum[0][:], ACT.Identity, bias=xsum[1][:])
+        V.scalar_tensor_tensor(gp[:], g[:], rz[:], p[:], ALU.mult, ALU.mult, accum_out=gs[:])
+        V.scalar_tensor_tensor(ds[:], pn[:], gs[:], gp[:], ALU.mult, ALU.subtract)
         e2 = f32("e2", I)
-        V.tensor_tensor(e2[:, cols[0]], ds[:].indirect(lists[0]), w[:, cols[0]], ALU.mult)
-        for h in range(NB):
-            V.scalar_tensor_tensor(halves(t)[h], pxs[h][:], xm[:], halves(ds)[h], ALU.subtract, ALU.mult, accum_out=ksum[h][:])
-        S.activation(ks[:], ksum[0][:], ACT.Identity, bias=ksum[1][:])
-        V.tensor_tensor(e2[:, cols[1]], ds[:].indirect(lists[1]), w[:, cols[1]], ALU.mult)
-        V.scalar_tensor_tensor(xds[:], npn[:], ks[:], t[:], ALU.mult, ALU.add)
+        V.tensor_tensor(e2[:], ds[:].indirect(offsets[:]), w[:], ALU.mult)
+        V.scalar_tensor_tensor(xp[:], xs[:], rz[:], p[:], ALU.mult, ALU.mult, accum_out=xm[:])
+        V.scalar_tensor_tensor(t[:], xs[:], xm[:], ds[:], ALU.subtract, ALU.mult, accum_out=ks[:])
+        V.scalar_tensor_tensor(xds[:], pn[:], ks[:], t[:], ALU.mult, ALU.subtract)
         e = f32("e", I)
-        for h in range(2):
-            V.tensor_tensor(e[:, cols[h]], xds[:].indirect(lists[h]), e2[:, cols[h]], ALU.add)
-        for h in range(2):
-            V.tensor_tensor(xs1[:].indirect(lists[h]), e[:, cols[h]], u[:, cols[h]], ALU.mult)
+        V.tensor_tensor(e[:], xds[:].indirect(offsets[:]), e2[:], ALU.add)
+        V.tensor_tensor(xs1[:].indirect(offsets[:]), e[:], u[:], ALU.mult)
 
-        pc = banks("c")
-        turn(pc, base_sb)
-        baset = f32("baset", T)
-        for h in range(NB):
-            S.copy(halves(baset)[h], pc[h][:])
-        py = banks("b")
-        turn(py, baset, stop=False)
+        base_s = f32("base_s", T, "xst")
+        S.activation(base_s[:], base_sb[:], ACT.Copy, scale=1.0 / 1024.0)
         pa = banks("a")
-        turn(pa, xds)
-        xdst = f32("xdst", T)
-        for h in range(NB):
-            S.activation(halves(xdst)[h], pa[h][:], ACT.Copy, scale=1024.0)
-        turn(py, xdst, start=False)
+        turn(pa, base_s, stop=False)
+        turn(pa, xds, start=False)
+        yt = copy_out("yt", pa, scale=1024.0)
+        py = banks("d")
+        turn(py, yt)
         res = f32("res", T)
         for k in range(NCH):
             h, c = divmod(k * CH, BANK)

@@ -152,17 +152,23 @@ def tile_attend_hvboost_heads_kernel(tc, query, keys_words, keys_scales, gout, v
         V.tensor_copy(bf[:].indirect(offsets[:]), bb[:])
 
         ta_sb = copy_out("ta_sb", pb)
-        v_bf = sb.tile([P, T + Q, PACK], BF16, name="v_bf", tag="a_g", align_bytes=64)
-        interleave(S.copy, v_bf[:, T:, :], go_raw[:])
-        for c in range(NCH):
-            interleave(S.copy, v_bf[:, c * CH:(c + 1) * CH, :], v_raw[c][:])
+        v = f32("v", I)
+        S.activation(v[:], th[:], ACT.Identity, scale=nhsteep[:], bias=hsteep[:])
+        g_bf = sb.tile([P, BANK, PACK], BF16, name="g_bf", align_bytes=64)
+        for c in range(2):
+            G.tensor_scalar(g_bf[:, c * CH:(c + 1) * CH, :], v_raw[c][:].rearrange("p j w -> p w j"), 1.0, 0.0, ALU.mult, ALU.add)
+        u = f32("u", I)
+        G.tensor_tensor(u[:], v[:], bb[:], ALU.mult)
+        s_bf = sb.tile([P, BANK + Q, PACK], BF16, name="s_bf", tag="a_g", align_bytes=64)
+        interleave(S.copy, s_bf[:, BANK:, :], go_raw[:])
+        for c in range(2):
+            interleave(S.copy, s_bf[:, c * CH:(c + 1) * CH, :], v_raw[2 + c][:])
         pb = banks("b")
         PE.matmul(pb[0][:, 0:P], lhsT=fac_rows[:], rhs=ident[:], is_transpose=True, start=True, stop=True)
         nfac_c = f32("nfac_c", T // P, "v_raw2")
         S.activation(nfac_c[:], pb[0][:, 0:T // P], ACT.Copy, scale=-1.0)
-        sq, v = f32("sq", I, "v_raw3"), f32("v", I)
-        S.activation(sq[:], th[:], ACT.Square)
-        S.activation(v[:], sq[:], ACT.Identity, scale=nhsteep[:], bias=hsteep[:])
+        r = f32("r", I, "go_raw")
+        S.activation(r[:], th[:], ACT.Copy, scale=nsteep[:])
 
         s = f32("s", T)
         V.tensor_tensor(s[:], a_sb[:], bf[:], ALU.add)
@@ -172,27 +178,28 @@ def tile_attend_hvboost_heads_kernel(tc, query, keys_words, keys_scales, gout, v
         z = f32("z", 1)
         S.activation(p[:], s[:], ACT.Exp, bias=nmax[:], accum_out=z[:])
 
-        codes = sb.tile([P, T + Q], U32, name="codes", tag="bf", align_bytes=64)
-        scales = sb.tile([P, T + Q], U8, name="scales", align_bytes=64)
-        v_codes, v_scales, go_codes, go_scales = codes[:, 0:T], scales[:, 0:T], codes[:, T:], scales[:, T:]
-        for piece in (slice(T, T + Q), slice(0, T)):
-            V.quantize_mx(out=codes[:, piece].bitcast(FP8X4), scales=scales[:, piece], in_=v_bf[:, piece, :].rearrange("p w j -> p (w j)"))
-        ta_g = f32("ta_g", I)
-        V.tensor_copy(ta_g[:], ta_sb[:].indirect(offsets[:]))
-        rz = f32("rz", 1)
-        V.reciprocal(rz[:], z[:])
-        u = f32("u", I, "a_sb")
-        V.tensor_tensor(by_quads(u[:]), by_quads(v[:]), hboost, ALU.mult)
-        w = f32("w", I, "v")
-        V.scalar_tensor_tensor(w[:], th[:], nsteep[:], ta_g[:], ALU.mult, ALU.mult)
-        V.tensor_tensor(xbf[:].indirect(offsets[:]), ta_g[:], u[:], ALU.mult)
+        go_codes = sb.tile([P, Q], U32, name="go_codes", align_bytes=64)
+        go_scales = sb.tile([P, Q], U8, name="go_scales", align_bytes=64)
+        v_codes = sb.tile([P, T], U32, name="v_codes", tag="bf", align_bytes=64)
+        v_scales = sb.tile([P, T], U8, name="v_scales", align_bytes=64)
+        for codes, scales, src in ((go_codes[:], go_scales[:], s_bf[:, BANK:, :]), (halves(v_codes)[0], halves(v_scales)[0], g_bf[:]),
+                                   (halves(v_codes)[1], halves(v_scales)[1], s_bf[:, 0:BANK, :])):
+            V.quantize_mx(out=codes.bitcast(FP8X4), scales=scales, in_=src.rearrange("p w j -> p (w j)"))
+        xbb = f32("xbb", I, "a_g")
+        V.tensor_tensor(xbb[:], ta_sb[:].indirect(offsets[:]), u[:], ALU.mult)
+        rz, minus1 = f32("rz", 1), f32("minus1", 1)
+        G.memset(minus1[:], -1.0)
+        G.tensor_tensor(rz[:], z[:], minus1[:], ALU.pow)
+        V.tensor_copy(xbf[:].indirect(offsets[:]), xbb[:])
+        w = f32("w", I)
+        G.tensor_tensor(w[:], xbb[:], r[:], ALU.mult)
 
         pa = banks("a")
         gt = f32("gt", T)
         for j in range(T // P):
             h, c = divmod(j, BLK)
             PE.matmul_mx(out=pa[h][:, c * P:(c + 1) * P], lhsT=v_codes[:, j * P:(j + 1) * P].bitcast(FP8X4), lhsT_scale=v_scales[:, j * P:(j + 1) * P],
-                         rhs=go_codes.bitcast(FP8X4), rhs_scale=go_scales, start=True, stop=True)
+                         rhs=go_codes[:].bitcast(FP8X4), rhs_scale=go_scales[:], start=True, stop=True)
         for j in range(T // P):
             h, c = divmod(j, BLK)
             S.activation(gt[:, j * P:(j + 1) * P], pa[h][:, c * P:(c + 1) * P], ACT.Copy, scale=nfac_c[:, j:j + 1])
@@ -220,8 +227,8 @@ def tile_attend_hvboost_heads_kernel(tc, query, keys_words, keys_scales, gout, v
         V.scalar_tensor_tensor(t[:], xs[:], xm[:], ds[:], ALU.subtract, ALU.mult, accum_out=ks[:])
         V.scalar_tensor_tensor(xds[:], pn[:], ks[:], t[:], ALU.mult, ALU.subtract)
         e = f32("e", I)
-        V.tensor_tensor(e[:], xds[:].indirect(offsets[:]), e2[:], ALU.add)
-        V.tensor_tensor(xs1[:].indirect(offsets[:]), e[:], u[:], ALU.mult)
+        V.tensor_tensor(e[:], xds[:].indirect(offsets[:]), u[:], ALU.mult)
+        V.tensor_tensor(xs1[:].indirect(offsets[:]), e[:], e2[:], ALU.add)
 
         base_s = f32("base_s", T, "xst")
         S.activation(base_s[:], base_sb[:], ACT.Copy, scale=1.0 / 1024.0)

@@ -4,7 +4,7 @@ import concourse.mybir as mybir
 from concourse.masks import make_identity
 
 D, E, T, Q, I = 512, 512, 1024, 128, 512
-FLOPS = 3 * 2 * 512 * Q * T
+FLOPS = 2 * Q * T * (D + D + E)
 
 F32 = mybir.dt.float32
 BF16 = mybir.dt.bfloat16
@@ -20,12 +20,16 @@ AX = mybir.AxisListType
 
 P = 128
 PACK = 4
+LINE = 4
 BANK = 512
-NB = T // BANK
-BLK = BANK // P
-CH = 256
-NCH = T // CH
+BANKS = T // BANK
+BLOCKS = BANK // P
+QUARTER = T // 4
+GROUP = 16
 HALF = I // 2
+QUADRANT = 32
+OUT_SCALE = 1024.0
+SATURATED = -30.0
 
 
 def tile_attend_hvboost_heads_kernel(tc, query, keys_words, keys_scales, gout, vals, steep, boost, fac, dquery, base, offs, out):
@@ -35,212 +39,214 @@ def tile_attend_hvboost_heads_kernel(tc, query, keys_words, keys_scales, gout, v
         sb = ctx.enter_context(tc.tile_pool(name="sb", bufs=1))
         ps = ctx.enter_context(tc.psum_pool(name="ps", bufs=1))
 
+        def halves(tile):
+            return [tile[:, h * BANK:(h + 1) * BANK] for h in range(BANKS)]
+
         def banks(tag):
-            return halves(ps.tile([P, NB * BANK], F32, name=tag))
+            return halves(ps.tile([P, BANKS * BANK], F32, name=tag))
 
         def f32(name, width, tag=None):
             return sb.tile([P, width], F32, name=name, tag=tag or name, align_bytes=64)
-
-        def interleave(copy, dst, src):
-            copy(dst.rearrange("p (c i) t -> p c t i", i=4), src.rearrange("p t (c i) -> p c t i", i=4))
 
         def load_rows(name, rows, width):
             raw = sb.tile([P, PACK, width], F32, name=name, align_bytes=64)
             nc.sync.dma_start(out=raw[:], in_=rows.rearrange("(p j) w -> p j w", j=PACK))
             return raw
 
-        def quantise(name, copy, raw, width):
-            grouped = sb.tile([P, width, PACK], BF16, name=name + "_bf", align_bytes=64)
-            codes = sb.tile([P, width], U32, name=name + "_codes", align_bytes=64)
+        def interleave(copy, dst, src):
+            copy(dst.rearrange("p (c i) j -> p c j i", i=LINE), src.rearrange("p j (c i) -> p c j i", i=LINE))
+
+        def quantise(codes, scales, grouped):
+            V.quantize_mx(out=codes.bitcast(FP8X4), scales=scales, in_=grouped.rearrange("p w j -> p (w j)"))
+
+        def mx_tiles(name, width, tag=None):
+            codes = sb.tile([P, width], U32, name=name + "_codes", tag=tag or name + "_codes", align_bytes=64)
             scales = sb.tile([P, width], U8, name=name + "_scales", align_bytes=64)
-            interleave(copy, grouped[:], raw[:])
-            V.quantize_mx(out=codes[:].bitcast(FP8X4), scales=scales[:], in_=grouped[:].rearrange("p w j -> p (w j)"))
             return codes, scales
 
         def turn(dst, src, start=True, stop=True):
             for j in range(T // P):
-                h, c = divmod(j, BLK)
+                h, c = divmod(j, BLOCKS)
                 PE.matmul(dst[h][:, c * P:(c + 1) * P], lhsT=src[:, j * P:(j + 1) * P], rhs=ident[:], is_transpose=True,
-                          start=(start and c == 0), stop=(stop and c == BLK - 1))
+                          start=(start and c == 0), stop=(stop and c == BLOCKS - 1))
 
-        def halves(tile):
-            return [tile[:, h * BANK:(h + 1) * BANK] for h in range(NB)]
-
-        def copy_out(name, src, scale=None, tag=None):
-            dst = f32(name, T, tag)
-            for h in range(NB):
-                if scale is None:
-                    S.copy(halves(dst)[h], src[h][:])
-                else:
-                    S.activation(halves(dst)[h], src[h][:], ACT.Copy, scale=scale)
+        def copy_out(name, src):
+            dst = f32(name, T)
+            for h in range(BANKS):
+                S.copy(halves(dst)[h], src[h])
             return dst
 
-        kscale = sb.tile([P, T], U8, name="kscale", align_bytes=64)
-        V.memset(kscale[:].bitcast(I32), 0)
+        key_scales = sb.tile([P, T], U8, name="key_scales", align_bytes=64)
+        V.memset(key_scales[:].bitcast(I32), 0)
         q_raw = load_rows("q_raw", query, Q)
-        kwords = sb.tile([P, 2 * T], U8, name="kwords", align_bytes=64)
-        nc.sync.dma_start(out=kwords[:].bitcast(I32), in_=keys_words[0].bitcast(I32))
-        for r in range(4):
-            nc.sync.dma_start(out=kscale[32 * r:32 * r + 4, :].bitcast(I32), in_=keys_scales[0, 4 * r:4 * r + 4, :].bitcast(I32))
+        key_words = sb.tile([P, 2 * T], U8, name="key_words", align_bytes=64)
+        nc.sync.dma_start(out=key_words[:].bitcast(I32), in_=keys_words[0].bitcast(I32))
+        for n in range(P // QUADRANT):
+            nc.sync.dma_start(out=key_scales[QUADRANT * n:QUADRANT * n + PACK, :].bitcast(I32),
+                              in_=keys_scales[0, PACK * n:PACK * (n + 1), :].bitcast(I32))
         dq_raw = load_rows("dq_raw", dquery, Q)
-        offsets = sb.tile([P, I // 16], U16, name="offsets")
+        offsets = sb.tile([P, I // GROUP], U16, name="offsets")
         nc.sync.dma_start(offsets[:], offs)
         ident = f32("ident", P)
         make_identity(nc, ident[:])
-        boost_c = f32("boost_c", PACK)
-        nc.sync.dma_start(out=boost_c[:], in_=boost[0].rearrange("(p c) -> p c", c=PACK))
-        steep_c = f32("steep_c", 1)
-        nc.sync.dma_start(out=steep_c[:], in_=steep)
+        boost_col = f32("boost_col", I // P)
+        nc.sync.dma_start(out=boost_col[:], in_=boost[0].rearrange("(p m) -> p m", m=I // P))
+        steep_col = f32("steep_col", 1)
+        nc.sync.dma_start(out=steep_col[:], in_=steep)
         fac_rows = f32("fac_rows", P)
         G.memset(fac_rows[:], 0.0)
-        v_raw = [load_rows("v_raw%d" % c, vals[:, c * CH:(c + 1) * CH], CH) for c in range(2)]
+        v_raw = [load_rows("v_raw%d" % c, vals[:, c * QUARTER:(c + 1) * QUARTER], QUARTER) for c in range(2)]
         go_raw = load_rows("go_raw", gout, Q)
-        v_raw = v_raw + [load_rows("v_raw%d" % c, vals[:, c * CH:(c + 1) * CH], CH) for c in range(2, NCH)]
+        v_raw = v_raw + [load_rows("v_raw%d" % c, vals[:, c * QUARTER:(c + 1) * QUARTER], QUARTER) for c in range(2, 4)]
         nc.sync.dma_start(out=fac_rows[0:T // P, :], in_=fac[0].rearrange("(j p) -> j p", p=P))
         base_sb = f32("base_sb", T)
         nc.sync.dma_start(out=base_sb[:], in_=base)
 
-        warm = f32("warm", 1)
-        V.memset(warm[:], 0.0)
-        warm_out = f32("warm_out", 1)
-        S.activation(warm_out[:], warm[:], ACT.Exp)
+        saturated, minus_one = f32("saturated", 1), f32("minus_one", 1)
+        V.memset(saturated[:], SATURATED)
+        S.activation(minus_one[:], saturated[:], ACT.Tanh)
         bf, xbf, xs1 = f32("bf", T), f32("xbf", T), f32("xs1", T)
         for window in (bf, xbf, xs1):
             V.memset(window[:], 0.0)
 
+        def scores(name, raw, dst, width):
+            grouped = sb.tile([P, Q, PACK], BF16, name=name + "_bf", align_bytes=64)
+            codes, scales = mx_tiles(name, Q)
+            interleave(V.tensor_copy, grouped[:], raw[:])
+            quantise(codes[:], scales[:], grouped[:])
+            for n, bank in enumerate(dst):
+                PE.matmul_mx(out=bank[:, 0:width], lhsT=codes[:].bitcast(FP8X4), lhsT_scale=scales[:],
+                             rhs=key_words[:, 2 * n * width:2 * (n + 1) * width].bitcast(FP4X4),
+                             rhs_scale=key_scales[:, n * width:(n + 1) * width], start=True, stop=True)
+
         def steep_times(name, factor):
             col = f32(name, 1)
-            S.activation(col[:], steep_c[:], ACT.Copy, scale=factor)
+            S.activation(col[:], steep_col[:], ACT.Copy, scale=factor)
             return col
 
-        def scores(codes, scales, dst, width):
-            for k, piece in enumerate(dst):
-                PE.matmul_mx(out=piece[:, 0:width], lhsT=codes[:].bitcast(FP8X4), lhsT_scale=scales[:],
-                             rhs=kwords[:, 2 * k * width:2 * (k + 1) * width].bitcast(FP4X4), rhs_scale=kscale[:, k * width:(k + 1) * width],
-                             start=True, stop=True)
+        a_banks = banks("pair0") + banks("pair1")
+        scores("q", q_raw, a_banks, QUARTER)
+        a = f32("a", T)
+        for n, bank in enumerate(a_banks):
+            (S.copy if n % 2 == 0 else V.tensor_copy)(a[:, n * QUARTER:(n + 1) * QUARTER], bank[:, 0:QUARTER])
 
-        pa = banks("a") + banks("d")
-        scores(*quantise("q", V.tensor_copy, q_raw, Q), pa, CH)
-        a_sb = f32("a_sb", T)
-        for k in range(NCH):
-            (S.copy if k % 2 == 0 else V.tensor_copy)(a_sb[:, k * CH:(k + 1) * CH], pa[k][:, 0:CH])
-        hboost_c = f32("hboost_c", PACK)
-        S.activation(hboost_c[:], boost_c[:], ACT.Copy, scale=0.5)
-        hsteep, nhsteep, nsteep = (steep_times(n, f) for n, f in (("hsteep", 0.5), ("nhsteep", -0.5), ("nsteep", -1.0)))
-        pc = banks("c")
-        for m in range(PACK):
-            PE.matmul(pc[0][:, m * P:(m + 1) * P], lhsT=hboost_c[:, m:m + 1].to_broadcast([P, P]), rhs=ident[:], is_transpose=True,
-                      start=(m == 0), stop=(m == PACK - 1))
-        hboost = pc[0][:].rearrange("p (m n) -> p n m", m=PACK)
-        pb = banks("b")
-        scores(*quantise("dq", V.tensor_copy, dq_raw, Q), pb, BANK)
+        half_boost_col = f32("half_boost_col", I // P)
+        S.activation(half_boost_col[:], boost_col[:], ACT.Copy, scale=0.5)
+        half_steep, minus_half_steep, minus_steep = steep_times("half_steep", 0.5), steep_times("minus_half_steep", -0.5), steep_times("minus_steep", -1.0)
+        boost_bank = ps.tile([P, I], F32, name="boost_bank")
+        for m in range(I // P):
+            PE.matmul(boost_bank[:, m * P:(m + 1) * P], lhsT=half_boost_col[:, m:m + 1].to_broadcast([P, P]), rhs=ident[:],
+                      is_transpose=True, start=(m == 0), stop=(m == I // P - 1))
+        half_boost = boost_bank[:].rearrange("p (m n) -> p n m", m=I // P)
 
-        a_g, th, bb = f32("a_g", I), f32("th", I), f32("bb", I)
-        lists = [offsets[:, h * HALF // 16:(h + 1) * HALF // 16] for h in range(2)]
-        cols = [slice(h * HALF, (h + 1) * HALF) for h in range(2)]
-        quads = [slice(h * HALF // PACK, (h + 1) * HALF // PACK) for h in range(2)]
+        ta_banks = banks("pair2")
+        scores("dq", dq_raw, ta_banks, BANK)
 
-        def by_quads(ap):
-            return ap.rearrange("p (n m) -> p n m", m=PACK)
-
+        a_listed, th, bb = f32("a_listed", I), f32("th", I), f32("bb", I)
         for h in range(2):
-            V.tensor_copy(a_g[:, cols[h]], a_sb[:].indirect(lists[h]))
+            V.tensor_copy(a_listed[:, h * HALF:(h + 1) * HALF], a[:].indirect(offsets[:, h * HALF // GROUP:(h + 1) * HALF // GROUP]))
         for h in range(2):
-            S.activation(th[:, cols[h]], a_g[:, cols[h]], ACT.Tanh, scale=hsteep[:])
+            S.activation(th[:, h * HALF:(h + 1) * HALF], a_listed[:, h * HALF:(h + 1) * HALF], ACT.Tanh, scale=half_steep[:])
+        th_by_n, bb_by_n = (tile[:].rearrange("p (n m) -> p n m", m=I // P) for tile in (th, bb))
         for h in range(2):
-            V.scalar_tensor_tensor(by_quads(bb[:, cols[h]]), by_quads(th[:, cols[h]]), 1.0, hboost[:, quads[h], :], ALU.add, ALU.mult)
+            ns = slice(h * P // 2, (h + 1) * P // 2)
+            V.scalar_tensor_tensor(bb_by_n[:, ns, :], th_by_n[:, ns, :], 1.0, half_boost[:, ns, :], ALU.add, ALU.mult)
         V.tensor_copy(bf[:].indirect(offsets[:]), bb[:])
 
-        ta_sb = copy_out("ta_sb", pb)
-        v = f32("v", I)
-        S.activation(v[:], th[:], ACT.Identity, scale=nhsteep[:], bias=hsteep[:])
-        g_bf = sb.tile([P, BANK, PACK], BF16, name="g_bf", align_bytes=64)
+        ta = copy_out("ta", ta_banks)
+        steep_rest = f32("steep_rest", I)
+        S.activation(steep_rest[:], th[:], ACT.Identity, scale=minus_half_steep[:], bias=half_steep[:])
+        first_bf = sb.tile([P, BANK, PACK], BF16, name="first_bf", align_bytes=64)
         for c in range(2):
-            G.tensor_scalar(g_bf[:, c * CH:(c + 1) * CH, :], v_raw[c][:].rearrange("p j w -> p w j"), 1.0, 0.0, ALU.mult, ALU.add)
+            G.tensor_scalar(first_bf[:, c * QUARTER:(c + 1) * QUARTER, :], v_raw[c][:].rearrange("p j w -> p w j"), 1.0, 0.0, ALU.mult, ALU.add)
         u = f32("u", I)
-        G.tensor_tensor(u[:], v[:], bb[:], ALU.mult)
-        s_bf = sb.tile([P, BANK + Q, PACK], BF16, name="s_bf", tag="a_g", align_bytes=64)
-        interleave(S.copy, s_bf[:, BANK:, :], go_raw[:])
+        G.tensor_tensor(u[:], steep_rest[:], bb[:], ALU.mult)
+        second_bf = sb.tile([P, BANK + Q, PACK], BF16, name="second_bf", tag="a_listed", align_bytes=64)
+        interleave(S.copy, second_bf[:, BANK:, :], go_raw[:])
         for c in range(2):
-            interleave(S.copy, s_bf[:, c * CH:(c + 1) * CH, :], v_raw[2 + c][:])
-        pb = banks("b")
-        PE.matmul(pb[0][:, 0:P], lhsT=fac_rows[:], rhs=ident[:], is_transpose=True, start=True, stop=True)
-        nfac_c = f32("nfac_c", T // P, "v_raw2")
-        S.activation(nfac_c[:], pb[0][:, 0:T // P], ACT.Copy, scale=-1.0)
-        r = f32("r", I, "go_raw")
-        S.activation(r[:], th[:], ACT.Copy, scale=nsteep[:])
+            interleave(S.copy, second_bf[:, c * QUARTER:(c + 1) * QUARTER, :], v_raw[2 + c][:])
+        fac_bank = banks("pair1")[0]
+        PE.matmul(fac_bank[:, 0:P], lhsT=fac_rows[:], rhs=ident[:], is_transpose=True, start=True, stop=True)
+        fac_col = f32("fac_col", T // P, "v_raw2")
+        S.copy(fac_col[:], fac_bank[:, 0:T // P])
+        tilt_and_p = f32("tilt_and_p", I + T, "v_raw3")
+        steep_tilt, p = tilt_and_p[:, 0:I], tilt_and_p[:, I:]
+        S.activation(steep_tilt, th[:], ACT.Copy, scale=minus_steep[:])
 
-        s = f32("s", T)
-        V.tensor_tensor(s[:], a_sb[:], bf[:], ALU.add)
-        nmax = f32("nmax", 1)
-        V.tensor_reduce(nmax[:], s[:], AX.X, ALU.max, negate=True)
-        p = f32("p", T, "v_raw3")
+        go_codes, go_scales = mx_tiles("go", Q)
+        v_codes, v_scales = mx_tiles("v", T, "bb")
+        quantise(halves(v_codes)[0], halves(v_scales)[0], first_bf[:])
+        quantise(go_codes[:], go_scales[:], second_bf[:, BANK:, :])
+        quantise(halves(v_codes)[1], halves(v_scales)[1], second_bf[:, 0:BANK, :])
+
+        s = f32("s", T, "a_listed")
+        V.tensor_tensor(s[:], a[:], bf[:], ALU.add)
+        minus_max = f32("minus_max", 1, "first_bf")
+        V.tensor_reduce(minus_max[:], s[:], AX.X, ALU.max, negate=True)
         z = f32("z", 1)
-        S.activation(p[:], s[:], ACT.Exp, bias=nmax[:], accum_out=z[:])
+        S.activation(p, s[:], ACT.Exp, bias=minus_max[:], accum_out=z[:])
 
-        go_codes = sb.tile([P, Q], U32, name="go_codes", align_bytes=64)
-        go_scales = sb.tile([P, Q], U8, name="go_scales", align_bytes=64)
-        v_codes = sb.tile([P, T], U32, name="v_codes", tag="bf", align_bytes=64)
-        v_scales = sb.tile([P, T], U8, name="v_scales", align_bytes=64)
-        for codes, scales, src in ((go_codes[:], go_scales[:], s_bf[:, BANK:, :]), (halves(v_codes)[0], halves(v_scales)[0], g_bf[:]),
-                                   (halves(v_codes)[1], halves(v_scales)[1], s_bf[:, 0:BANK, :])):
-            V.quantize_mx(out=codes.bitcast(FP8X4), scales=scales, in_=src.rearrange("p w j -> p (w j)"))
-        xbb = f32("xbb", I, "a_g")
-        V.tensor_tensor(xbb[:], ta_sb[:].indirect(offsets[:]), u[:], ALU.mult)
-        rz, minus1 = f32("rz", 1), f32("minus1", 1)
-        G.memset(minus1[:], -1.0)
-        G.tensor_tensor(rz[:], z[:], minus1[:], ALU.pow)
+        xbb = f32("xbb", I, "a")
+        V.tensor_tensor(xbb[:], ta[:].indirect(offsets[:]), u[:], ALU.mult)
+        rz = f32("rz", 1)
+        G.tensor_tensor(rz[:], z[:], minus_one[:], ALU.pow)
         V.tensor_copy(xbf[:].indirect(offsets[:]), xbb[:])
         w = f32("w", I)
-        G.tensor_tensor(w[:], xbb[:], r[:], ALU.mult)
+        G.tensor_tensor(w[:], xbb[:], steep_tilt, ALU.mult)
 
-        pa = banks("a")
-        gt = f32("gt", T)
+        c0_banks = banks("pair0")
+        g_turned = f32("g_turned", T)
         for j in range(T // P):
-            h, c = divmod(j, BLK)
-            PE.matmul_mx(out=pa[h][:, c * P:(c + 1) * P], lhsT=v_codes[:, j * P:(j + 1) * P].bitcast(FP8X4), lhsT_scale=v_scales[:, j * P:(j + 1) * P],
-                         rhs=go_codes[:].bitcast(FP8X4), rhs_scale=go_scales[:], start=True, stop=True)
+            h, c = divmod(j, BLOCKS)
+            PE.matmul_mx(out=c0_banks[h][:, c * P:(c + 1) * P], lhsT=v_codes[:, j * P:(j + 1) * P].bitcast(FP8X4),
+                         lhsT_scale=v_scales[:, j * P:(j + 1) * P], rhs=go_codes[:].bitcast(FP8X4), rhs_scale=go_scales[:],
+                         start=True, stop=True)
         for j in range(T // P):
-            h, c = divmod(j, BLK)
-            S.activation(gt[:, j * P:(j + 1) * P], pa[h][:, c * P:(c + 1) * P], ACT.Copy, scale=nfac_c[:, j:j + 1])
-        pg = banks("d")
-        turn(pg, gt)
-        g = copy_out("g", pg)
-        pn = f32("pn", T, "gt")
-        S.activation(pn[:], p[:], ACT.Copy, scale=rz[:])
+            h, c = divmod(j, BLOCKS)
+            S.activation(g_turned[:, j * P:(j + 1) * P], c0_banks[h][:, c * P:(c + 1) * P], ACT.Copy, scale=fac_col[:, j:j + 1])
+        g_banks = banks("pair1")
+        turn(g_banks, g_turned)
+        g = copy_out("g", g_banks)
+        pn = f32("pn", T, "g_turned")
+        S.activation(pn[:], p, ACT.Copy, scale=rz[:])
 
-        pa = banks("a")
-        turn(pa, ta_sb, stop=False)
-        turn(pa, xbf, start=False)
-        xst = copy_out("xst", pa, scale=-1.0)
-        pxs = banks("b")
-        turn(pxs, xst)
-        xs = copy_out("xs", pxs)
+        g_p, g_pn = f32("g_p", T), f32("g_pn", T)
+        gs_part = [f32("gs_part%d" % h, 1) for h in range(BANKS)]
+        gs = f32("gs", 1)
+        for h in range(BANKS):
+            G.tensor_tensor(halves(g_p)[h], halves(g)[h], halves(p)[h], ALU.mult)
+            S.activation(halves(g_pn)[h], halves(g_p)[h], ACT.Copy, scale=rz[:], accum_out=gs_part[h][:])
+        S.activation(gs[:], gs_part[0][:], ACT.Identity, bias=gs_part[1][:])
 
-        gp, ds, xp, t, xds = f32("gp", T), f32("ds", T), f32("xp", T), f32("t", T), f32("xds", T)
-        gs, xm, ks = f32("gs", 1), f32("xm", 1), f32("ks", 1)
-        V.scalar_tensor_tensor(gp[:], g[:], rz[:], p[:], ALU.mult, ALU.mult, accum_out=gs[:])
-        V.scalar_tensor_tensor(ds[:], pn[:], gs[:], gp[:], ALU.mult, ALU.subtract)
-        e2 = f32("e2", I)
-        V.tensor_tensor(e2[:], ds[:].indirect(offsets[:]), w[:], ALU.mult)
-        V.scalar_tensor_tensor(xp[:], xs[:], rz[:], p[:], ALU.mult, ALU.mult, accum_out=xm[:])
-        V.scalar_tensor_tensor(t[:], xs[:], xm[:], ds[:], ALU.subtract, ALU.mult, accum_out=ks[:])
-        V.scalar_tensor_tensor(xds[:], pn[:], ks[:], t[:], ALU.mult, ALU.subtract)
-        e = f32("e", I)
-        V.tensor_tensor(e[:], xds[:].indirect(offsets[:]), u[:], ALU.mult)
-        V.tensor_tensor(xs1[:].indirect(offsets[:]), e[:], e2[:], ALU.add)
+        minus_xs, minus_xs_pn, ds, minus_xs_ds, xds = (f32(name, T) for name in ("minus_xs", "minus_xs_pn", "ds", "minus_xs_ds", "xds"))
+        minus_xm, minus_ks = f32("minus_xm", 1), f32("minus_ks", 1)
+        for h in range(BANKS):
+            V.scalar_tensor_tensor(halves(minus_xs)[h], halves(xbf)[h], -1.0, ta_banks[h], ALU.mult, ALU.subtract)
+        V.scalar_tensor_tensor(minus_xs_pn[:], minus_xs[:], rz[:], p, ALU.mult, ALU.mult, accum_out=minus_xm[:])
+        V.scalar_tensor_tensor(ds[:], g[:], gs[:], pn[:], ALU.subtract, ALU.mult)
+        V.scalar_tensor_tensor(minus_xs_ds[:], minus_xs[:], minus_xm[:], ds[:], ALU.subtract, ALU.mult, accum_out=minus_ks[:])
+        ds_w = f32("ds_w", I)
+        V.tensor_tensor(ds_w[:], ds[:].indirect(offsets[:]), w[:], ALU.mult)
+        V.scalar_tensor_tensor(xds[:], pn[:], minus_ks[:], minus_xs_ds[:], ALU.mult, ALU.subtract)
 
-        base_s = f32("base_s", T, "xst")
-        S.activation(base_s[:], base_sb[:], ACT.Copy, scale=1.0 / 1024.0)
-        pa = banks("a")
-        turn(pa, base_s, stop=False)
-        turn(pa, xds, start=False)
-        yt = copy_out("yt", pa, scale=1024.0)
-        py = banks("d")
-        turn(py, yt)
-        res = f32("res", T)
-        for k in range(NCH):
-            h, c = divmod(k * CH, BANK)
-            piece = slice(k * CH, (k + 1) * CH)
-            V.scalar_tensor_tensor(res[:, piece], xs1[:, piece], 1024.0, py[h][:, c:c + CH], ALU.mult, ALU.add)
-            (nc.sync if k % 2 == 0 else nc.scalar).dma_start(out=out[:, piece], in_=res[:, piece])
+        xds_u = f32("xds_u", I)
+        V.tensor_tensor(xds_u[:], xds[:].indirect(offsets[:]), u[:], ALU.mult)
+        V.tensor_tensor(xs1[:].indirect(offsets[:]), xds_u[:], ds_w[:], ALU.add)
+
+        base_scaled = f32("base_scaled", T, "g_p")
+        S.activation(base_scaled[:], base_sb[:], ACT.Copy, scale=1.0 / OUT_SCALE)
+        sum_banks = banks("pair0")
+        turn(sum_banks, base_scaled, stop=False)
+        turn(sum_banks, xds, start=False)
+        y_turned = f32("y_turned", T)
+        for h in range(BANKS):
+            S.activation(halves(y_turned)[h], sum_banks[h], ACT.Copy, scale=OUT_SCALE)
+        y_banks = banks("pair1")
+        turn(y_banks, y_turned)
+
+        result = f32("result", T)
+        for n in range(T // QUARTER):
+            h, first = divmod(n * QUARTER, BANK)
+            piece = slice(n * QUARTER, (n + 1) * QUARTER)
+            V.scalar_tensor_tensor(result[:, piece], xs1[:, piece], OUT_SCALE, y_banks[h][:, first:first + QUARTER], ALU.mult, ALU.add)
+            (nc.sync if n % 2 == 0 else nc.scalar).dma_start(out=out[:, piece], in_=result[:, piece])

from contextlib import ExitStack

import concourse.mybir as mybir
from concourse.masks import make_identity

D, E, T, Q, I = 512, 512, 1024, 128, 512
FLOPS = 2 * Q * T * (D + D + E)

F32 = mybir.dt.float32
BF16 = mybir.dt.bfloat16
U32 = mybir.dt.uint32
I32 = mybir.dt.int32
U16 = mybir.dt.uint16
U8 = mybir.dt.uint8
FP8X4 = mybir.dt.float8_e4m3fn_x4
FP4X4 = mybir.dt.float4_e2m1fn_x4
ALU = mybir.AluOpType
ACT = mybir.ActivationFunctionType
AX = mybir.AxisListType

P = 128
PACK = 4
LINE = 4
BANK = 512
BANKS = T // BANK
BLOCKS = BANK // P
QUARTER = T // 4
GROUP = 16
HALF = I // 2
QUADRANT = 32
OUT_SCALE = 1024.0
SATURATED = -30.0


def tile_attend_hvboost_heads_kernel(tc, query, keys_words, keys_scales, gout, vals, steep, boost, fac, dquery, base, offs, out):
    nc = tc.nc
    V, S, G, PE = nc.vector, nc.scalar, nc.gpsimd, nc.tensor
    with ExitStack() as ctx:
        sb = ctx.enter_context(tc.tile_pool(name="sb", bufs=1))
        ps = ctx.enter_context(tc.psum_pool(name="ps", bufs=1))

        def halves(tile):
            return [tile[:, h * BANK:(h + 1) * BANK] for h in range(BANKS)]

        def banks(tag):
            return halves(ps.tile([P, BANKS * BANK], F32, name=tag))

        def f32(name, width, tag=None):
            return sb.tile([P, width], F32, name=name, tag=tag or name, align_bytes=64)

        def load_rows(name, rows, width):
            raw = sb.tile([P, PACK, width], F32, name=name, align_bytes=64)
            nc.sync.dma_start(out=raw[:], in_=rows.rearrange("(p j) w -> p j w", j=PACK))
            return raw

        def interleave(copy, dst, src):
            copy(dst.rearrange("p (c i) j -> p c j i", i=LINE), src.rearrange("p j (c i) -> p c j i", i=LINE))

        def quantise(codes, scales, grouped):
            V.quantize_mx(out=codes.bitcast(FP8X4), scales=scales, in_=grouped.rearrange("p w j -> p (w j)"))

        def mx_tiles(name, width, tag=None):
            codes = sb.tile([P, width], U32, name=name + "_codes", tag=tag or name + "_codes", align_bytes=64)
            scales = sb.tile([P, width], U8, name=name + "_scales", align_bytes=64)
            return codes, scales

        def turn(dst, src, start=True, stop=True):
            for j in range(T // P):
                h, c = divmod(j, BLOCKS)
                PE.matmul(dst[h][:, c * P:(c + 1) * P], lhsT=src[:, j * P:(j + 1) * P], rhs=ident[:], is_transpose=True,
                          start=(start and c == 0), stop=(stop and c == BLOCKS - 1))

        def copy_out(name, src):
            dst = f32(name, T)
            for h in range(BANKS):
                S.copy(halves(dst)[h], src[h])
            return dst

        key_scales = sb.tile([P, T], U8, name="key_scales", align_bytes=64)
        V.memset(key_scales[:].bitcast(I32), 0)
        q_raw = load_rows("q_raw", query, Q)
        key_words = sb.tile([P, 2 * T], U8, name="key_words", align_bytes=64)
        nc.sync.dma_start(out=key_words[:].bitcast(I32), in_=keys_words[0].bitcast(I32))
        for n in range(P // QUADRANT):
            nc.sync.dma_start(out=key_scales[QUADRANT * n:QUADRANT * n + PACK, :].bitcast(I32),
                              in_=keys_scales[0, PACK * n:PACK * (n + 1), :].bitcast(I32))
        dq_raw = load_rows("dq_raw", dquery, Q)
        offsets = sb.tile([P, I // GROUP], U16, name="offsets")
        nc.sync.dma_start(offsets[:], offs)
        ident = f32("ident", P)
        make_identity(nc, ident[:])
        boost_col = f32("boost_col", I // P)
        nc.sync.dma_start(out=boost_col[:], in_=boost[0].rearrange("(p m) -> p m", m=I // P))
        steep_col = f32("steep_col", 1)
        nc.sync.dma_start(out=steep_col[:], in_=steep)
        fac_rows = f32("fac_rows", P)
        G.memset(fac_rows[:], 0.0)
        v_raw = [load_rows("v_raw%d" % c, vals[:, c * QUARTER:(c + 1) * QUARTER], QUARTER) for c in range(2)]
        go_raw = load_rows("go_raw", gout, Q)
        v_raw = v_raw + [load_rows("v_raw%d" % c, vals[:, c * QUARTER:(c + 1) * QUARTER], QUARTER) for c in range(2, 4)]
        nc.sync.dma_start(out=fac_rows[0:T // P, :], in_=fac[0].rearrange("(j p) -> j p", p=P))
        base_sb = f32("base_sb", T)
        nc.sync.dma_start(out=base_sb[:], in_=base)

        saturated, minus_one = f32("saturated", 1), f32("minus_one", 1)
        V.memset(saturated[:], SATURATED)
        S.activation(minus_one[:], saturated[:], ACT.Tanh)
        bf, xbf, xs1 = f32("bf", T), f32("xbf", T), f32("xs1", T)
        for window in (bf, xbf, xs1):
            V.memset(window[:], 0.0)

        def scores(name, raw, dst, width):
            grouped = sb.tile([P, Q, PACK], BF16, name=name + "_bf", align_bytes=64)
            codes, scales = mx_tiles(name, Q)
            interleave(V.tensor_copy, grouped[:], raw[:])
            quantise(codes[:], scales[:], grouped[:])
            for n, bank in enumerate(dst):
                PE.matmul_mx(out=bank[:, 0:width], lhsT=codes[:].bitcast(FP8X4), lhsT_scale=scales[:],
                             rhs=key_words[:, 2 * n * width:2 * (n + 1) * width].bitcast(FP4X4),
                             rhs_scale=key_scales[:, n * width:(n + 1) * width], start=True, stop=True)

        def steep_times(name, factor):
            col = f32(name, 1)
            S.activation(col[:], steep_col[:], ACT.Copy, scale=factor)
            return col

        a_banks = banks("pair0") + banks("pair1")
        scores("q", q_raw, a_banks, QUARTER)
        a = f32("a", T)
        for n, bank in enumerate(a_banks):
            (S.copy if n % 2 == 0 else V.tensor_copy)(a[:, n * QUARTER:(n + 1) * QUARTER], bank[:, 0:QUARTER])

        half_boost_col = f32("half_boost_col", I // P)
        S.activation(half_boost_col[:], boost_col[:], ACT.Copy, scale=0.5)
        half_steep, minus_half_steep, minus_steep = steep_times("half_steep", 0.5), steep_times("minus_half_steep", -0.5), steep_times("minus_steep", -1.0)
        boost_bank = ps.tile([P, I], F32, name="boost_bank")
        for m in range(I // P):
            PE.matmul(boost_bank[:, m * P:(m + 1) * P], lhsT=half_boost_col[:, m:m + 1].to_broadcast([P, P]), rhs=ident[:],
                      is_transpose=True, start=(m == 0), stop=(m == I // P - 1))
        half_boost = boost_bank[:].rearrange("p (m n) -> p n m", m=I // P)

        ta_banks = banks("pair2")
        scores("dq", dq_raw, ta_banks, BANK)

        a_listed, th, bb = f32("a_listed", I), f32("th", I), f32("bb", I)
        for h in range(2):
            V.tensor_copy(a_listed[:, h * HALF:(h + 1) * HALF], a[:].indirect(offsets[:, h * HALF // GROUP:(h + 1) * HALF // GROUP]))
        for h in range(2):
            S.activation(th[:, h * HALF:(h + 1) * HALF], a_listed[:, h * HALF:(h + 1) * HALF], ACT.Tanh, scale=half_steep[:])
        th_by_n, bb_by_n = (tile[:].rearrange("p (n m) -> p n m", m=I // P) for tile in (th, bb))
        for h in range(2):
            ns = slice(h * P // 2, (h + 1) * P // 2)
            V.scalar_tensor_tensor(bb_by_n[:, ns, :], th_by_n[:, ns, :], 1.0, half_boost[:, ns, :], ALU.add, ALU.mult)
        V.tensor_copy(bf[:].indirect(offsets[:]), bb[:])

        ta = copy_out("ta", ta_banks)
        steep_rest = f32("steep_rest", I)
        S.activation(steep_rest[:], th[:], ACT.Identity, scale=minus_half_steep[:], bias=half_steep[:])
        first_bf = sb.tile([P, BANK, PACK], BF16, name="first_bf", align_bytes=64)
        for c in range(2):
            G.tensor_scalar(first_bf[:, c * QUARTER:(c + 1) * QUARTER, :], v_raw[c][:].rearrange("p j w -> p w j"), 1.0, 0.0, ALU.mult, ALU.add)
        u = f32("u", I)
        G.tensor_tensor(u[:], steep_rest[:], bb[:], ALU.mult)
        second_bf = sb.tile([P, BANK + Q, PACK], BF16, name="second_bf", tag="a_listed", align_bytes=64)
        interleave(S.copy, second_bf[:, BANK:, :], go_raw[:])
        for c in range(2):
            interleave(S.copy, second_bf[:, c * QUARTER:(c + 1) * QUARTER, :], v_raw[2 + c][:])
        fac_bank = banks("pair1")[0]
        PE.matmul(fac_bank[:, 0:P], lhsT=fac_rows[:], rhs=ident[:], is_transpose=True, start=True, stop=True)
        fac_col = f32("fac_col", T // P, "v_raw2")
        S.copy(fac_col[:], fac_bank[:, 0:T // P])
        tilt_and_p = f32("tilt_and_p", I + T, "v_raw3")
        steep_tilt, p = tilt_and_p[:, 0:I], tilt_and_p[:, I:]
        S.activation(steep_tilt, th[:], ACT.Copy, scale=minus_steep[:])

        go_codes, go_scales = mx_tiles("go", Q)
        v_codes, v_scales = mx_tiles("v", T, "bb")
        quantise(halves(v_codes)[0], halves(v_scales)[0], first_bf[:])
        quantise(go_codes[:], go_scales[:], second_bf[:, BANK:, :])
        quantise(halves(v_codes)[1], halves(v_scales)[1], second_bf[:, 0:BANK, :])

        s = f32("s", T, "a_listed")
        V.tensor_tensor(s[:], a[:], bf[:], ALU.add)
        minus_max = f32("minus_max", 1, "first_bf")
        V.tensor_reduce(minus_max[:], s[:], AX.X, ALU.max, negate=True)
        z = f32("z", 1)
        S.activation(p, s[:], ACT.Exp, bias=minus_max[:], accum_out=z[:])

        xbb = f32("xbb", I, "a")
        V.tensor_tensor(xbb[:], ta[:].indirect(offsets[:]), u[:], ALU.mult)
        rz = f32("rz", 1)
        G.tensor_tensor(rz[:], z[:], minus_one[:], ALU.pow)
        V.tensor_copy(xbf[:].indirect(offsets[:]), xbb[:])
        w = f32("w", I)
        G.tensor_tensor(w[:], xbb[:], steep_tilt, ALU.mult)

        c0_banks = banks("pair0")
        g_turned = f32("g_turned", T)
        for j in range(T // P):
            h, c = divmod(j, BLOCKS)
            PE.matmul_mx(out=c0_banks[h][:, c * P:(c + 1) * P], lhsT=v_codes[:, j * P:(j + 1) * P].bitcast(FP8X4),
                         lhsT_scale=v_scales[:, j * P:(j + 1) * P], rhs=go_codes[:].bitcast(FP8X4), rhs_scale=go_scales[:],
                         start=True, stop=True)
        for j in range(T // P):
            h, c = divmod(j, BLOCKS)
            S.activation(g_turned[:, j * P:(j + 1) * P], c0_banks[h][:, c * P:(c + 1) * P], ACT.Copy, scale=fac_col[:, j:j + 1])
        g_banks = banks("pair1")
        turn(g_banks, g_turned)
        g = copy_out("g", g_banks)
        pn = f32("pn", T, "g_turned")
        S.activation(pn[:], p, ACT.Copy, scale=rz[:])

        g_p, g_pn = f32("g_p", T), f32("g_pn", T)
        gs_part = [f32("gs_part%d" % h, 1) for h in range(BANKS)]
        gs = f32("gs", 1)
        for h in range(BANKS):
            G.tensor_tensor(halves(g_p)[h], halves(g)[h], halves(p)[h], ALU.mult)
            S.activation(halves(g_pn)[h], halves(g_p)[h], ACT.Copy, scale=rz[:], accum_out=gs_part[h][:])
        S.activation(gs[:], gs_part[0][:], ACT.Identity, bias=gs_part[1][:])

        minus_xs, minus_xs_pn, ds, minus_xs_ds, xds = (f32(name, T) for name in ("minus_xs", "minus_xs_pn", "ds", "minus_xs_ds", "xds"))
        minus_xm, minus_ks = f32("minus_xm", 1), f32("minus_ks", 1)
        for h in range(BANKS):
            V.scalar_tensor_tensor(halves(minus_xs)[h], halves(xbf)[h], -1.0, ta_banks[h], ALU.mult, ALU.subtract)
        V.scalar_tensor_tensor(minus_xs_pn[:], minus_xs[:], rz[:], p, ALU.mult, ALU.mult, accum_out=minus_xm[:])
        V.scalar_tensor_tensor(ds[:], g[:], gs[:], pn[:], ALU.subtract, ALU.mult)
        V.scalar_tensor_tensor(minus_xs_ds[:], minus_xs[:], minus_xm[:], ds[:], ALU.subtract, ALU.mult, accum_out=minus_ks[:])
        ds_w = f32("ds_w", I)
        V.tensor_tensor(ds_w[:], ds[:].indirect(offsets[:]), w[:], ALU.mult)
        V.scalar_tensor_tensor(xds[:], pn[:], minus_ks[:], minus_xs_ds[:], ALU.mult, ALU.subtract)

        xds_u = f32("xds_u", I)
        V.tensor_tensor(xds_u[:], xds[:].indirect(offsets[:]), u[:], ALU.mult)
        V.tensor_tensor(xs1[:].indirect(offsets[:]), xds_u[:], ds_w[:], ALU.add)

        base_scaled = f32("base_scaled", T, "g_p")
        S.activation(base_scaled[:], base_sb[:], ACT.Copy, scale=1.0 / OUT_SCALE)
        sum_banks = banks("pair0")
        turn(sum_banks, base_scaled, stop=False)
        turn(sum_banks, xds, start=False)
        y_turned = f32("y_turned", T)
        for h in range(BANKS):
            S.activation(halves(y_turned)[h], sum_banks[h], ACT.Copy, scale=OUT_SCALE)
        y_banks = banks("pair1")
        turn(y_banks, y_turned)

        result = f32("result", T)
        for n in range(T // QUARTER):
            h, first = divmod(n * QUARTER, BANK)
            piece = slice(n * QUARTER, (n + 1) * QUARTER)
            V.scalar_tensor_tensor(result[:, piece], xs1[:, piece], OUT_SCALE, y_banks[h][:, first:first + QUARTER], ALU.mult, ALU.add)
            (nc.sync if n % 2 == 0 else nc.scalar).dma_start(out=out[:, piece], in_=result[:, piece])
